import numpy as np
import ml_dtypes


def mxq(x, axis, fmt="e4m3"):
    dtype, down = {"e4m3": (ml_dtypes.float8_e4m3fn, 7), "e5m2": (ml_dtypes.float8_e5m2, 14)}[fmt]
    v = np.moveaxis(np.asarray(x, np.float32).astype(ml_dtypes.bfloat16).astype(np.float64), axis, -1)
    blocks = v.reshape(v.shape[:-1] + (-1, 32))
    amax = np.abs(blocks).max(-1, keepdims=True)
    byte = np.maximum(np.where(amax > 0, np.frexp(amax)[1] - 1 + 127, 0) - down, 1)
    scale = np.exp2(byte - 127.0)
    codes = (blocks / scale).astype(np.float32).astype(dtype).astype(np.float64)
    return np.moveaxis((codes * scale).reshape(v.shape), -1, axis)


WIDE = False


def mx_kscale(k):
    if not WIDE:
        return np.ones(k)
    levels = np.array([10, -10, 5, -5, 0])
    if k % 512:
        return np.exp2(np.random.permutation(np.resize(levels, k // 32))).repeat(32)
    a = np.empty((k // 512, 16))
    for p in range(k // 512):
        a[p, :8] = np.random.permutation(np.resize(levels, 8))
        for g in range(8):
            far = levels[np.abs(levels - a[p, g]) >= 10]
            a[p, g + 8] = far[np.random.randint(len(far))]
    return np.exp2(a.ravel()).repeat(32)


def f64(x):
    return np.asarray(x).astype(np.float64)


def striped(idx):
    return np.tile(idx.reshape(-1, 16).T, (8, 1)).astype(np.uint16)


def unstriped(offs):
    return offs[:16].T.reshape(-1).astype(np.int64)


E2M1 = np.array([0.0, 0.5, 1.0, 1.5, 2.0, 3.0, 4.0, 6.0, -0.0, -0.5, -1.0, -1.5, -2.0, -3.0, -4.0, -6.0])


def pack_weight(w, fmt):
    k, n = w.shape
    w = f64(np.asarray(w, np.float32).astype(ml_dtypes.bfloat16)).reshape(k // 32, 32, n)
    amax = np.abs(w).max(1)
    if fmt == "e4m3":
        byte = np.frexp(amax)[1] - 1 + 127 - 7
    else:
        mant, ex = np.frexp(amax / 6.0)
        byte = np.where(mant > 0.5, ex, ex - 1) + 127
    byte = np.clip(np.where(amax > 0, byte, 1), 1, 254)
    scaled = (w * np.exp2(127.0 - byte)[:, None, :]).reshape(k, n).astype(np.float32)
    by_word = np.ascontiguousarray(scaled.reshape(k // 512, 128, 4, n).transpose(0, 1, 3, 2))
    if fmt == "e4m3":
        words = by_word.astype(ml_dtypes.float8_e4m3fn).view(np.uint8)
    else:
        c = by_word.astype(ml_dtypes.float4_e2m1fn).view(np.uint8) & 0xF
        words = (c[..., 0::2] | (c[..., 1::2] << 4)).reshape(k // 512, 128, 2 * n)
    return np.ascontiguousarray(words), np.ascontiguousarray(byte.astype(np.uint8).reshape(k // 512, 16, n))


def unpack_weight(words, scales, fmt):
    g, _, n = scales.shape
    words = np.ascontiguousarray(words).reshape(g, 128, n, -1)
    if fmt == "e4m3":
        vals = words.view(ml_dtypes.float8_e4m3fn).astype(np.float64)
    else:
        nib = np.empty((g, 128, n, 4), np.uint8)
        nib[..., 0::2] = words & 0xF
        nib[..., 1::2] = words >> 4
        vals = E2M1[nib]
    vals = vals * np.repeat(np.exp2(scales.astype(np.float64) - 127.0), 8, axis=1)[..., None]
    return vals.transpose(0, 1, 3, 2).reshape(g * 512, n)


def silu(v):
    return v / (1.0 + np.exp(-np.maximum(v, -700.0)))


K, T, E, C, N = 2560, 384, 12, 128, 256
TOP = 4
K8 = 1024


def by_expert(wq, xq):
    return np.concatenate([wq[e].T @ xq[:, e * C:(e + 1) * C] for e in range(E)], axis=1)


def setup_inputs():
    n = np.random.standard_normal
    s = mx_kscale(K)[:, None]
    deal = np.repeat(np.arange(E), C).reshape(TOP, T)[:, np.random.permutation(T)]
    deal = np.take_along_axis(deal, np.argsort(np.random.rand(TOP, T), axis=0), axis=0)
    for _ in range(8):
        s_, t_ = np.random.permutation(T).reshape(2, -1); r = np.random.randint(TOP, size=T // 2); x, y = deal[r, s_].copy(), deal[r, t_].copy()
        ok = ~((deal[:, s_] == y).any(0) | (deal[:, t_] == x).any(0)); deal[r[ok], s_[ok]] = y[ok]; deal[r[ok], t_[ok]] = x[ok]
    order = np.lexsort((np.random.rand(TOP * T), deal.reshape(-1)))
    slot_token = order % T; pos = np.empty(TOP * T, np.int64); pos[order] = np.arange(TOP * T); pos = pos.reshape(TOP, T)
    g = np.random.uniform(0.5, 1.5, (TOP, T)); g = g / g.sum(0)
    w = n((E, K, N)) / np.sqrt(K) / s[None]
    w8 = [pack_weight(m[:K8], "e4m3") for m in w]
    w4 = [pack_weight(m[K8:], "e2m1") for m in w]
    return {
        "xT": (n((K, T)) * s).astype(np.float32),
        "w8_words": np.stack([m[0] for m in w8]),
        "w8_scales": np.stack([m[1] for m in w8]),
        "w4_words": np.stack([m[0] for m in w4]),
        "w4_scales": np.stack([m[1] for m in w4]),
        "b": (0.3 * n((N, E))).astype(np.float32),
        "gate": np.stack([np.tile(r, (N, 1)) for r in g]).astype(np.float32),
        "offs": striped(slot_token),
        "pos1": striped(pos[0]),
        "pos2": striped(pos[1]),
        "pos3": striped(pos[2]),
        "pos4": striped(pos[3]),
    }


def reference(xT, w8_words, w8_scales, w4_words, w4_scales, b, gate, offs, pos1, pos2, pos3, pos4):
    idx = unstriped(offs)
    w = np.stack([np.concatenate([unpack_weight(w8_words[e], w8_scales[e], "e4m3"), unpack_weight(w4_words[e], w4_scales[e], "e2m1")]) for e in range(E)])
    xq = mxq(f64(xT)[:, idx], 0, "e4m3")
    y = by_expert(w, xq)
    y = silu(y + np.repeat(f64(b), C, axis=1))
    return sum(f64(gate[r]) * y[:, unstriped(p)] for r, p in enumerate((pos1, pos2, pos3, pos4)))

@@ -1,0 +1,212 @@
+from contextlib import ExitStack
+
+import concourse.mybir as mybir
+
+K, T, E, C, N, TOP = 2560, 384, 12, 128, 256, 4
+S = E * C
+P = 128
+PASSES, PASSES8 = 5, 2
+PASSES4 = PASSES - PASSES8
+HALVES = N // P
+FLOPS = 2 * S * K * N
+BYTES = 4 * K * T + E * N * (PASSES8 * (512 + 16) + PASSES4 * (256 + 16)) + 4 * N * E + 4 * TOP * T + 2 * P * (S + TOP * T) // 16 + 4 * N * T
+
+F32 = mybir.dt.float32
+BF16 = mybir.dt.bfloat16
+I32 = mybir.dt.int32
+U32 = mybir.dt.uint32
+U16 = mybir.dt.uint16
+U8 = mybir.dt.uint8
+FP8X4 = mybir.dt.float8_e4m3fn_x4
+FP4X4 = mybir.dt.float4_e2m1fn_x4
+COPY = mybir.ActivationFunctionType.Copy
+SILU = mybir.ActivationFunctionType.Silu
+MULT = mybir.AluOpType.mult
+ADD = mybir.AluOpType.add
+
+WINDOW = 1024
+PAD = WINDOW - T
+PLANE_ROW = (4, 8, 0, 12, 0)
+PACK_OF = (0, 0, 0, 0, 1)
+PACKS = 2
+SHIFTED = 3
+BATCHES = ((0, 4), (4, 8), (8, 10), (10, 12))
+
+
+def tile_moe_tk_lin_silu_kernel(tc, xT, w8_words, w8_scales, w4_words, w4_scales, b, gate, offs, pos1, pos2, pos3, pos4, out):
+    nc = tc.nc
+    with ExitStack() as ctx:
+        lists = ctx.enter_context(tc.tile_pool(name="lists", bufs=1))
+        keep = ctx.enter_context(tc.tile_pool(name="keep", bufs=1))
+        psum = ctx.enter_context(tc.psum_pool(name="psum", bufs=8))
+
+        offs_sb = lists.tile([P, S // 16], U16, name="offs_sb")
+        pos_sb = [lists.tile([P, T // 16], U16, name=f"pos_sb{r}") for r in range(TOP)]
+
+        words = keep.tile([P, PASSES * T + PAD], I32, name="words", align_bytes=64)
+        planes = keep.tile([P, PACKS * T + PAD], U8, name="planes", align_bytes=64)
+        w8 = keep.tile([P, E * PASSES8, 4 * N], U8, name="w8", align_bytes=64)
+        w4 = keep.tile([P, E * PASSES4, 2 * N], U8, name="w4", align_bytes=64)
+        w8s = keep.tile([P, E * PASSES8, N], U8, name="w8s", align_bytes=64)
+        w4s = keep.tile([P, E * PASSES4, N], U8, name="w4s", align_bytes=64)
+        bias = keep.tile([P, HALVES, E], F32, name="bias")
+        gates = keep.tile([P, TOP, T], F32, name="gates")
+        raw = [keep.tile([P, 4, T], F32, name=f"raw{a}") for a in range(PASSES)]
+        grouped = [keep.tile([P, T, 4], BF16, name=f"grouped{a}", align_bytes=64) for a in range(PASSES)]
+        slot_words = [keep.tile([P, S], U32, name=f"slot_words{a}", align_bytes=64) for a in range(PASSES)]
+        slot_planes = [keep.tile([P, S], U8, name=f"slot_planes{q}", align_bytes=64) for q in range(PACKS)]
+        shifted = keep.tile([P, S], U8, name="shifted", align_bytes=64)
+        y = [keep.tile([P, S], F32, name=f"y{h}") for h in range(HALVES)]
+        dummy = keep.tile([P, 1], F32, name="dummy")
+
+        x_rows = xT.rearrange("(a p j) t -> a p j t", p=P, j=4)
+        nc.sync.dma_start(out=raw[0][:, :, 0:256], in_=x_rows[0][:, :, 0:256])
+        nc.sync.dma_start(out=raw[0][:, :, 256:T], in_=x_rows[0][:, :, 256:T])
+        nc.sync.dma_start(offs_sb[:], offs)
+        for a in range(1, PASSES):
+            nc.sync.dma_start(out=raw[a][:], in_=x_rows[a])
+
+        nc.vector.memset(dummy[:], 0.0)
+        nc.scalar.activation(dummy[:], dummy[:], SILU)
+        nc.vector.memset(planes[:].bitcast(I32), 0)
+        nc.vector.memset(words[:, PASSES * T :], 0)
+        nc.vector.memset(shifted[:].bitcast(I32), 0)
+        nc.vector.memset(w8s[:].rearrange("p e n -> p (e n)").bitcast(I32), 0)
+        nc.gpsimd.memset(w4s[:].rearrange("p e n -> p (e n)").bitcast(I32), 0)
+
+        w8_rows = w8_words.rearrange("e a p n r -> p (e a) (n r)").bitcast(I32)
+        w4_rows = w4_words.rearrange("e a p n -> p (e a) n").bitcast(I32)
+        w8s_rows = w8_scales.rearrange("e a q n -> q (e a) n").bitcast(I32)
+        w4s_rows = w4_scales.rearrange("e a q n -> q (e a) n").bitcast(I32)
+        for q in range(4):
+            nc.sync.dma_start(out=w8s[32 * q : 32 * q + 4].bitcast(I32), in_=w8s_rows[4 * q : 4 * q + 4])
+            nc.sync.dma_start(out=w4s[32 * q : 32 * q + 4].bitcast(I32), in_=w4s_rows[4 * q : 4 * q + 4])
+        for r, pos in enumerate((pos1, pos2, pos3, pos4)):
+            nc.sync.dma_start(pos_sb[r][:], pos)
+        nc.sync.dma_start(out=bias[:], in_=b.rearrange("(h p) e -> p h e", p=P))
+        def load_weights(e0, e1):
+            r8 = slice(e0 * PASSES8, e1 * PASSES8)
+            r4 = slice(e0 * PASSES4, e1 * PASSES4)
+            nc.sync.dma_start(out=w8[:, r8].bitcast(I32), in_=w8_rows[:, r8])
+            nc.sync.dma_start(out=w4[:, r4].bitcast(I32), in_=w4_rows[:, r4])
+
+        load_weights(*BATCHES[0])
+
+        def interleave_scalar(a, t0, t1):
+            nc.scalar.activation(grouped[a][:, t0:t1, :], raw[a][:, :, t0:t1].rearrange("p j t -> p t j"), COPY)
+
+        def interleave_vector(a, t0, t1):
+            nc.vector.tensor_copy(out=grouped[a][:, t0:t1, :], in_=raw[a][:, :, t0:t1].rearrange("p j t -> p t j"))
+
+        def word_column(a):
+            return (PASSES - 1 - a) * T
+
+        def plane_column(q):
+            return (PACKS - 1 - q) * T
+
+        def quantise(a):
+            for t0, t1 in ((0, 256), (256, T)):
+                w0, s0 = word_column(a), plane_column(PACK_OF[a])
+                nc.vector.quantize_mx(
+                    out=words[:, w0 + t0 : w0 + t1].bitcast(FP8X4),
+                    scales=planes[PLANE_ROW[a] : P, s0 + t0 : s0 + t1],
+                    in_=grouped[a][:, t0:t1, :].rearrange("p t j -> p (t j)"),
+                )
+
+        def gather_words(a, j0, j1):
+            w0 = word_column(a)
+            nc.vector.tensor_copy(
+                out=slot_words[a][:, j0:j1],
+                in_=words[:, w0 : w0 + WINDOW].bitcast(U32).indirect(offs_sb[:, j0 // 16 : j1 // 16]),
+            )
+
+        def gather_planes(q, j0, j1):
+            s0 = plane_column(q)
+            nc.vector.tensor_copy(
+                out=slot_planes[q][:, j0:j1],
+                in_=planes[:, s0 : s0 + WINDOW].indirect(offs_sb[:, j0 // 16 : j1 // 16]),
+            )
+
+        def shift_planes(j0, j1):
+            k = PLANE_ROW[SHIFTED]
+            nc.sync.dma_start(
+                out=shifted[0:100, j0:j1].bitcast(I32),
+                in_=slot_planes[PACK_OF[SHIFTED]][k : k + 100, j0:j1].bitcast(I32),
+            )
+
+        def multiply(acc, a, e, h):
+            cols = slice(e * C, (e + 1) * C)
+            if a < PASSES8:
+                i = e * PASSES8 + a
+                lhsT = w8[:, i, 4 * P * h : 4 * P * (h + 1)].bitcast(FP8X4)
+                lhsT_scale = w8s[:, i, P * h : P * (h + 1)]
+            else:
+                i = e * PASSES4 + a - PASSES8
+                lhsT = w4[:, i, 2 * P * h : 2 * P * (h + 1)].bitcast(FP4X4)
+                lhsT_scale = w4s[:, i, P * h : P * (h + 1)]
+            nc.tensor.matmul_mx(
+                out=acc[:],
+                lhsT=lhsT,
+                lhsT_scale=lhsT_scale,
+                rhs=slot_words[a][:, cols].bitcast(FP8X4),
+                rhs_scale=shifted[:, cols] if a == SHIFTED else slot_planes[PACK_OF[a]][PLANE_ROW[a] : P, cols],
+                start=(a == 0),
+                stop=(a == PASSES - 1),
+            )
+
+        interleave_scalar(0, 0, 128)
+        interleave_vector(0, 128, 256)
+        interleave_vector(0, 256, T)
+        for a in range(1, PASSES):
+            interleave_scalar(a, 0, T)
+        quantise(0)
+        gather_words(0, 0, S // 2)
+        quantise(1)
+        gather_words(0, S // 2, S)
+        gather_words(1, 0, S // 2)
+        quantise(2)
+        gather_words(1, S // 2, S)
+        quantise(3)
+
+        for i, (e0, e1) in enumerate(BATCHES):
+            j0, j1 = e0 * C, e1 * C
+            gather_words(2, j0, j1)
+            gather_planes(0, j0, j1)
+            shift_planes(j0, j1)
+            if e0 == 0:
+                quantise(4)
+            if j1 < S:
+                load_weights(*BATCHES[i + 1])
+            else:
+                nc.sync.dma_start(out=gates[:], in_=gate[:, 0:P, :].rearrange("r p t -> p r t"))
+            gather_words(3, j0, j1)
+            gather_planes(1, j0, j1)
+            accs = {}
+            for e in range(e0, e1):
+                for h in range(HALVES):
+                    accs[e, h] = psum.tile([P, C], F32, name="acc")
+            for a in range(PASSES - 1):
+                for e in range(e0, e1):
+                    for h in range(HALVES):
+                        multiply(accs[e, h], a, e, h)
+            step = C if j1 == S else j1 - j0
+            for j in range(j0, j1, step):
+                gather_words(PASSES - 1, j, j + step)
+                for e in range(j // C, (j + step) // C):
+                    for h in range(HALVES):
+                        multiply(accs[e, h], PASSES - 1, e, h)
+                        nc.scalar.activation(y[h][:, e * C : (e + 1) * C], accs[e, h][:], SILU, bias=bias[:, h, e : e + 1])
+
+        for h in range(HALVES):
+            picked = []
+            for r in range(TOP):
+                part = keep.tile([P, T], F32, name=f"part{h}_{r}")
+                nc.vector.tensor_tensor(part[:], y[h][:].indirect(pos_sb[r][:]), gates[:, r, :], MULT)
+                picked.append(part)
+            low = keep.tile([P, T], F32, name=f"low{h}")
+            high = keep.tile([P, T], F32, name=f"high{h}")
+            total = keep.tile([P, T], F32, name=f"total{h}")
+            nc.vector.tensor_tensor(low[:], picked[0][:], picked[1][:], ADD)
+            nc.vector.tensor_tensor(high[:], picked[2][:], picked[3][:], ADD)
+            nc.vector.tensor_tensor(total[:], low[:], high[:], ADD)
+            nc.sync.dma_start(out=out[h * P : (h + 1) * P, :], in_=total[:])

@@ -26,11 +26,13 @@ ADD = mybir.AluOpType.add
 
 WINDOW = 1024
 PAD = WINDOW - T
-PLANE_ROW = (4, 8, 0, 12, 0)
+PLANE_WINDOW = 1536
+W8_ROW = 4
+PLANE_ROW = (4, 12, 0, 8, 0)
 PACK_OF = (0, 0, 0, 0, 1)
 PACKS = 2
 SHIFTED = 3
-BATCHES = ((0, 4), (4, 8), (8, 10), (10, 12))
+BATCHES = ((0, 4), (4, 8), (8, 12))
 
 
 def tile_moe_tk_lin_silu_kernel(tc, xT, w8_words, w8_scales, w4_words, w4_scales, b, gate, offs, pos1, pos2, pos3, pos4, out):
@@ -44,7 +46,7 @@ def tile_moe_tk_lin_silu_kernel(tc, xT, w8_words, w8_scales, w4_words, w4_scales
         pos_sb = [lists.tile([P, T // 16], U16, name=f"pos_sb{r}") for r in range(TOP)]
 
         words = keep.tile([P, PASSES * T + PAD], I32, name="words", align_bytes=64)
-        planes = keep.tile([P, PACKS * T + PAD], U8, name="planes", align_bytes=64)
+        planes = keep.tile([P, (PACKS - 1) * T + PLANE_WINDOW], U8, name="planes", align_bytes=64)
         w8 = keep.tile([P, E * PASSES8, 4 * N], U8, name="w8", align_bytes=64)
         w4 = keep.tile([P, E * PASSES4, 2 * N], U8, name="w4", align_bytes=64)
         w8s = keep.tile([P, E * PASSES8, N], U8, name="w8s", align_bytes=64)
@@ -53,7 +55,7 @@ def tile_moe_tk_lin_silu_kernel(tc, xT, w8_words, w8_scales, w4_words, w4_scales
         gates = keep.tile([P, TOP, T], F32, name="gates")
         raw = [keep.tile([P, 4, T], F32, name=f"raw{a}") for a in range(PASSES)]
         grouped = [keep.tile([P, T, 4], BF16, name=f"grouped{a}", align_bytes=64) for a in range(PASSES)]
-        slot_words = [keep.tile([P, S], U32, name=f"slot_words{a}", align_bytes=64) for a in range(PASSES)]
+        first_words = keep.tile([P, S], U32, name="first_words", align_bytes=64)
         slot_planes = [keep.tile([P, S], U8, name=f"slot_planes{q}", align_bytes=64) for q in range(PACKS)]
         shifted = keep.tile([P, S], U8, name="shifted", align_bytes=64)
         y = [keep.tile([P, S], F32, name=f"y{h}") for h in range(HALVES)]
@@ -63,34 +65,43 @@ def tile_moe_tk_lin_silu_kernel(tc, xT, w8_words, w8_scales, w4_words, w4_scales
         nc.sync.dma_start(out=raw[0][:, :, 0:256], in_=x_rows[0][:, :, 0:256])
         nc.sync.dma_start(out=raw[0][:, :, 256:T], in_=x_rows[0][:, :, 256:T])
         nc.sync.dma_start(offs_sb[:], offs)
-        for a in range(1, PASSES):
-            nc.sync.dma_start(out=raw[a][:], in_=x_rows[a])
 
         nc.vector.memset(dummy[:], 0.0)
         nc.scalar.activation(dummy[:], dummy[:], SILU)
         nc.vector.memset(planes[:].bitcast(I32), 0)
         nc.vector.memset(words[:, PASSES * T :], 0)
         nc.vector.memset(shifted[:].bitcast(I32), 0)
-        nc.vector.memset(w8s[:].rearrange("p e n -> p (e n)").bitcast(I32), 0)
-        nc.gpsimd.memset(w4s[:].rearrange("p e n -> p (e n)").bitcast(I32), 0)
+        nc.vector.memset(w4s[:].rearrange("p e n -> p (e n)").bitcast(I32), 0)
+        nc.gpsimd.memset(w8s[:].rearrange("p e n -> p (e n)").bitcast(I32), 0)
 
         w8_rows = w8_words.rearrange("e a p n r -> p (e a) (n r)").bitcast(I32)
         w4_rows = w4_words.rearrange("e a p n -> p (e a) n").bitcast(I32)
         w8s_rows = w8_scales.rearrange("e a q n -> q (e a) n").bitcast(I32)
         w4s_rows = w4_scales.rearrange("e a q n -> q (e a) n").bitcast(I32)
-        for q in range(4):
-            nc.sync.dma_start(out=w8s[32 * q : 32 * q + 4].bitcast(I32), in_=w8s_rows[4 * q : 4 * q + 4])
-            nc.sync.dma_start(out=w4s[32 * q : 32 * q + 4].bitcast(I32), in_=w4s_rows[4 * q : 4 * q + 4])
+        def load_w8(e0, e1):
+            rows = slice(e0 * PASSES8, e1 * PASSES8)
+            nc.sync.dma_start(out=w8[:, rows].bitcast(I32), in_=w8_rows[:, rows])
+
+        def load_w4(e0, e1):
+            rows = slice(e0 * PASSES4, e1 * PASSES4)
+            nc.sync.dma_start(out=w4[:, rows].bitcast(I32), in_=w4_rows[:, rows])
+
+        for r in range(4):
+            nc.gpsimd.dma_start(out=w8s[W8_ROW + r : P : 32].bitcast(I32), in_=w8s_rows[r:16:4])
+        for r in range(4):
+            nc.gpsimd.dma_start(out=w4s[r:P:32].bitcast(I32), in_=w4s_rows[r:16:4])
+        for a in range(1, PASSES):
+            nc.sync.dma_start(out=raw[a][:], in_=x_rows[a])
+        nc.sync.dma_start(out=bias[:], in_=b.rearrange("(h p) e -> p h e", p=P))
+        load_w8(0, 4)
+        load_w4(0, 4)
+        load_w8(4, 8)
+        load_w4(4, 8)
         for r, pos in enumerate((pos1, pos2, pos3, pos4)):
             nc.sync.dma_start(pos_sb[r][:], pos)
-        nc.sync.dma_start(out=bias[:], in_=b.rearrange("(h p) e -> p h e", p=P))
-        def load_weights(e0, e1):
-            r8 = slice(e0 * PASSES8, e1 * PASSES8)
-            r4 = slice(e0 * PASSES4, e1 * PASSES4)
-            nc.sync.dma_start(out=w8[:, r8].bitcast(I32), in_=w8_rows[:, r8])
-            nc.sync.dma_start(out=w4[:, r4].bitcast(I32), in_=w4_rows[:, r4])
-
-        load_weights(*BATCHES[0])
+        load_w8(8, 12)
+        load_w4(8, 12)
+        nc.sync.dma_start(out=gates[:], in_=gate[:, 0:P, :].rearrange("r p t -> p r t"))
 
         def interleave_scalar(a, t0, t1):
             nc.scalar.activation(grouped[a][:, t0:t1, :], raw[a][:, :, t0:t1].rearrange("p j t -> p t j"), COPY)
@@ -113,10 +124,10 @@ def tile_moe_tk_lin_silu_kernel(tc, xT, w8_words, w8_scales, w4_words, w4_scales
                     in_=grouped[a][:, t0:t1, :].rearrange("p t j -> p (t j)"),
                 )
 
-        def gather_words(a, j0, j1):
+        def gather_words(a, dst, j0, j1):
             w0 = word_column(a)
             nc.vector.tensor_copy(
-                out=slot_words[a][:, j0:j1],
+                out=dst,
                 in_=words[:, w0 : w0 + WINDOW].bitcast(U32).indirect(offs_sb[:, j0 // 16 : j1 // 16]),
             )
 
@@ -124,22 +135,22 @@ def tile_moe_tk_lin_silu_kernel(tc, xT, w8_words, w8_scales, w4_words, w4_scales
             s0 = plane_column(q)
             nc.vector.tensor_copy(
                 out=slot_planes[q][:, j0:j1],
-                in_=planes[:, s0 : s0 + WINDOW].indirect(offs_sb[:, j0 // 16 : j1 // 16]),
+                in_=planes[:, s0 : s0 + (WINDOW if j1 - j0 <= 512 else PLANE_WINDOW)].indirect(offs_sb[:, j0 // 16 : j1 // 16]),
             )
 
         def shift_planes(j0, j1):
             k = PLANE_ROW[SHIFTED]
-            nc.sync.dma_start(
+            nc.gpsimd.dma_start(
                 out=shifted[0:100, j0:j1].bitcast(I32),
                 in_=slot_planes[PACK_OF[SHIFTED]][k : k + 100, j0:j1].bitcast(I32),
             )
 
-        def multiply(acc, a, e, h):
+        def multiply(acc, a, e, h, moving):
             cols = slice(e * C, (e + 1) * C)
             if a < PASSES8:
                 i = e * PASSES8 + a
                 lhsT = w8[:, i, 4 * P * h : 4 * P * (h + 1)].bitcast(FP8X4)
-                lhsT_scale = w8s[:, i, P * h : P * (h + 1)]
+                lhsT_scale = w8s[W8_ROW:P, i, P * h : P * (h + 1)]
             else:
                 i = e * PASSES4 + a - PASSES8
                 lhsT = w4[:, i, 2 * P * h : 2 * P * (h + 1)].bitcast(FP4X4)
@@ -148,7 +159,7 @@ def tile_moe_tk_lin_silu_kernel(tc, xT, w8_words, w8_scales, w4_words, w4_scales
                 out=acc[:],
                 lhsT=lhsT,
                 lhsT_scale=lhsT_scale,
-                rhs=slot_words[a][:, cols].bitcast(FP8X4),
+                rhs=moving.bitcast(FP8X4),
                 rhs_scale=shifted[:, cols] if a == SHIFTED else slot_planes[PACK_OF[a]][PLANE_ROW[a] : P, cols],
                 start=(a == 0),
                 stop=(a == PASSES - 1),
@@ -160,27 +171,33 @@ def tile_moe_tk_lin_silu_kernel(tc, xT, w8_words, w8_scales, w4_words, w4_scales
         for a in range(1, PASSES):
             interleave_scalar(a, 0, T)
         quantise(0)
-        gather_words(0, 0, S // 2)
+        gather_words(0, first_words[:, 0 : S // 2], 0, S // 2)
         quantise(1)
-        gather_words(0, S // 2, S)
-        gather_words(1, 0, S // 2)
-        quantise(2)
-        gather_words(1, S // 2, S)
-        quantise(3)
+        gather_words(0, first_words[:, S // 2 : S], S // 2, S)
 
-        for i, (e0, e1) in enumerate(BATCHES):
+        for e0, e1 in BATCHES:
             j0, j1 = e0 * C, e1 * C
-            gather_words(2, j0, j1)
-            gather_planes(0, j0, j1)
-            shift_planes(j0, j1)
+            if e0 > 0:
+                if e0 == BATCHES[1][0]:
+                    gather_planes(0, j0, S)
+                    shift_planes(j0, S)
+                    gather_planes(1, j0, S)
+            batch_words = {0: first_words[:, j0:j1]}
+            for a in range(1, PASSES):
+                tile = keep.tile([P, j1 - j0], U32, name=f"batch_words{a}", align_bytes=64)
+                batch_words[a] = tile[:]
+            gather_words(1, batch_words[1], j0, j1)
+            if e0 == 0:
+                quantise(2)
+            gather_words(2, batch_words[2], j0, j1)
+            if e0 == 0:
+                quantise(3)
+                gather_planes(0, j0, j1)
+                shift_planes(j0, j1)
+            gather_words(3, batch_words[3], j0, j1)
             if e0 == 0:
                 quantise(4)
-            if j1 < S:
-                load_weights(*BATCHES[i + 1])
-            else:
-                nc.sync.dma_start(out=gates[:], in_=gate[:, 0:P, :].rearrange("r p t -> p r t"))
-            gather_words(3, j0, j1)
-            gather_planes(1, j0, j1)
+                gather_planes(1, j0, j1)
             accs = {}
             for e in range(e0, e1):
                 for h in range(HALVES):
@@ -188,25 +205,41 @@ def tile_moe_tk_lin_silu_kernel(tc, xT, w8_words, w8_scales, w4_words, w4_scales
             for a in range(PASSES - 1):
                 for e in range(e0, e1):
                     for h in range(HALVES):
-                        multiply(accs[e, h], a, e, h)
-            step = C if j1 == S else j1 - j0
-            for j in range(j0, j1, step):
-                gather_words(PASSES - 1, j, j + step)
-                for e in range(j // C, (j + step) // C):
+                        multiply(accs[e, h], a, e, h, batch_words[a][:, (e - e0) * C : (e - e0 + 1) * C])
+            for f0, f1 in ((e0, e1),) if e1 < E else ((e0, e0 + 2), (e0 + 2, e0 + 3), (e0 + 3, e1)):
+                gather_words(4, batch_words[4][:, (f0 - e0) * C : (f1 - e0) * C], f0 * C, f1 * C)
+                for e in range(f0, f1):
                     for h in range(HALVES):
-                        multiply(accs[e, h], PASSES - 1, e, h)
+                        multiply(accs[e, h], 4, e, h, batch_words[4][:, (e - e0) * C : (e - e0 + 1) * C])
                         nc.scalar.activation(y[h][:, e * C : (e + 1) * C], accs[e, h][:], SILU, bias=bias[:, h, e : e + 1])
 
-        for h in range(HALVES):
-            picked = []
-            for r in range(TOP):
-                part = keep.tile([P, T], F32, name=f"part{h}_{r}")
-                nc.vector.tensor_tensor(part[:], y[h][:].indirect(pos_sb[r][:]), gates[:, r, :], MULT)
-                picked.append(part)
-            low = keep.tile([P, T], F32, name=f"low{h}")
-            high = keep.tile([P, T], F32, name=f"high{h}")
-            total = keep.tile([P, T], F32, name=f"total{h}")
-            nc.vector.tensor_tensor(low[:], picked[0][:], picked[1][:], ADD)
-            nc.vector.tensor_tensor(high[:], picked[2][:], picked[3][:], ADD)
-            nc.vector.tensor_tensor(total[:], low[:], high[:], ADD)
-            nc.sync.dma_start(out=out[h * P : (h + 1) * P, :], in_=total[:])
+        part = [[keep.tile([P, T], F32, name=f"part{h}_{r}") for r in range(TOP)] for h in range(HALVES)]
+        low = [keep.tile([P, T], F32, name=f"low{h}") for h in range(HALVES)]
+        three = [keep.tile([P, T], F32, name=f"three{h}") for h in range(HALVES)]
+        total = [keep.tile([P, T], F32, name=f"total{h}") for h in range(HALVES)]
+
+        def pick(h, r):
+            nc.vector.tensor_tensor(part[h][r][:], y[h][:].indirect(pos_sb[r][:]), gates[:, r, :], MULT)
+
+        def add(dst, a, b):
+            nc.vector.tensor_tensor(dst[:], a[:], b[:], ADD)
+
+        def store(h):
+            nc.sync.dma_start(out=out[h * P : (h + 1) * P, :], in_=total[h][:])
+
+        pick(0, 0)
+        pick(0, 1)
+        pick(0, 2)
+        add(low[0], part[0][0], part[0][1])
+        pick(0, 3)
+        add(three[0], low[0], part[0][2])
+        pick(1, 0)
+        add(total[0], three[0], part[0][3])
+        store(0)
+        pick(1, 1)
+        pick(1, 2)
+        add(low[1], part[1][0], part[1][1])
+        pick(1, 3)
+        add(three[1], low[1], part[1][2])
+        add(total[1], three[1], part[1][3])
+        store(1)

@@ -32,6 +32,7 @@ PLANE_ROW = (4, 12, 0, 8, 0)
 PACK_OF = (0, 0, 0, 0, 1)
 PACKS = 2
 SHIFTED = 3
+EARLY = 2
 BATCHES = ((0, 4), (4, 8), (8, 12))
 
 
@@ -55,7 +56,7 @@ def tile_moe_tk_lin_silu_kernel(tc, xT, w8_words, w8_scales, w4_words, w4_scales
         gates = keep.tile([P, TOP, T], F32, name="gates")
         raw = [keep.tile([P, 4, T], F32, name=f"raw{a}") for a in range(PASSES)]
         grouped = [keep.tile([P, T, 4], BF16, name=f"grouped{a}", align_bytes=64) for a in range(PASSES)]
-        first_words = keep.tile([P, S], U32, name="first_words", align_bytes=64)
+        early_words = [keep.tile([P, S], U32, name=f"early_words{a}", align_bytes=64) for a in range(EARLY)]
         slot_planes = [keep.tile([P, S], U8, name=f"slot_planes{q}", align_bytes=64) for q in range(PACKS)]
         shifted = keep.tile([P, S], U8, name="shifted", align_bytes=64)
         y = [keep.tile([P, S], F32, name=f"y{h}") for h in range(HALVES)]
@@ -70,9 +71,9 @@ def tile_moe_tk_lin_silu_kernel(tc, xT, w8_words, w8_scales, w4_words, w4_scales
         nc.scalar.activation(dummy[:], dummy[:], SILU)
         nc.vector.memset(planes[:].bitcast(I32), 0)
         nc.vector.memset(words[:, PASSES * T :], 0)
-        nc.vector.memset(shifted[:].bitcast(I32), 0)
+        nc.vector.memset(w8s[:].rearrange("p e n -> p (e n)").bitcast(I32), 0)
         nc.vector.memset(w4s[:].rearrange("p e n -> p (e n)").bitcast(I32), 0)
-        nc.gpsimd.memset(w8s[:].rearrange("p e n -> p (e n)").bitcast(I32), 0)
+        nc.vector.memset(shifted[:].bitcast(I32), 0)
 
         w8_rows = w8_words.rearrange("e a p n r -> p (e a) (n r)").bitcast(I32)
         w4_rows = w4_words.rearrange("e a p n -> p (e a) n").bitcast(I32)
@@ -92,16 +93,17 @@ def tile_moe_tk_lin_silu_kernel(tc, xT, w8_words, w8_scales, w4_words, w4_scales
             nc.gpsimd.dma_start(out=w4s[r:P:32].bitcast(I32), in_=w4s_rows[r:16:4])
         for a in range(1, PASSES):
             nc.sync.dma_start(out=raw[a][:], in_=x_rows[a])
-        nc.sync.dma_start(out=bias[:], in_=b.rearrange("(h p) e -> p h e", p=P))
         load_w8(0, 4)
         load_w4(0, 4)
+        nc.sync.dma_start(out=bias[:], in_=b.rearrange("(h p) e -> p h e", p=P))
         load_w8(4, 8)
         load_w4(4, 8)
         for r, pos in enumerate((pos1, pos2, pos3, pos4)):
             nc.sync.dma_start(pos_sb[r][:], pos)
         load_w8(8, 12)
         load_w4(8, 12)
-        nc.sync.dma_start(out=gates[:], in_=gate[:, 0:P, :].rearrange("r p t -> p r t"))
+        for r in range(TOP):
+            nc.sync.dma_start(out=gates[:, r, :], in_=gate[r, 0:P, :])
 
         def interleave_scalar(a, t0, t1):
             nc.scalar.activation(grouped[a][:, t0:t1, :], raw[a][:, :, t0:t1].rearrange("p j t -> p t j"), COPY)
@@ -171,32 +173,30 @@ def tile_moe_tk_lin_silu_kernel(tc, xT, w8_words, w8_scales, w4_words, w4_scales
         for a in range(1, PASSES):
             interleave_scalar(a, 0, T)
         quantise(0)
-        gather_words(0, first_words[:, 0 : S // 2], 0, S // 2)
-        quantise(1)
-        gather_words(0, first_words[:, S // 2 : S], S // 2, S)
+        for a in range(EARLY):
+            for j in range(0, S, S // 2):
+                gather_words(a, early_words[a][:, j : j + S // 2], j, j + S // 2)
+            quantise(a + 1)
+        quantise(3)
 
         for e0, e1 in BATCHES:
             j0, j1 = e0 * C, e1 * C
+            if e0 == BATCHES[1][0]:
+                gather_planes(0, j0, S)
+                shift_planes(j0, S)
             if e0 > 0:
-                if e0 == BATCHES[1][0]:
-                    gather_planes(0, j0, S)
-                    shift_planes(j0, S)
-                    gather_planes(1, j0, S)
-            batch_words = {0: first_words[:, j0:j1]}
-            for a in range(1, PASSES):
+                gather_planes(1, j0, j1)
+            batch_words = {a: early_words[a][:, j0:j1] for a in range(EARLY)}
+            for a in range(EARLY, PASSES):
                 tile = keep.tile([P, j1 - j0], U32, name=f"batch_words{a}", align_bytes=64)
                 batch_words[a] = tile[:]
-            gather_words(1, batch_words[1], j0, j1)
-            if e0 == 0:
-                quantise(2)
             gather_words(2, batch_words[2], j0, j1)
             if e0 == 0:
-                quantise(3)
                 gather_planes(0, j0, j1)
                 shift_planes(j0, j1)
+                quantise(4)
             gather_words(3, batch_words[3], j0, j1)
             if e0 == 0:
-                quantise(4)
                 gather_planes(1, j0, j1)
             accs = {}
             for e in range(e0, e1):
@@ -221,11 +221,11 @@ def tile_moe_tk_lin_silu_kernel(tc, xT, w8_words, w8_scales, w4_words, w4_scales
         def pick(h, r):
             nc.vector.tensor_tensor(part[h][r][:], y[h][:].indirect(pos_sb[r][:]), gates[:, r, :], MULT)
 
-        def add(dst, a, b):
-            nc.vector.tensor_tensor(dst[:], a[:], b[:], ADD)
+        def add(dst, a, b, t0=0, t1=T):
+            nc.vector.tensor_tensor(dst[:, t0:t1], a[:, t0:t1], b[:, t0:t1], ADD)
 
-        def store(h):
-            nc.sync.dma_start(out=out[h * P : (h + 1) * P, :], in_=total[h][:])
+        def store(h, t0=0, t1=T):
+            nc.sync.dma_start(out=out[h * P : (h + 1) * P, t0:t1], in_=total[h][:, t0:t1])
 
         pick(0, 0)
         pick(0, 1)
@@ -241,5 +241,6 @@ def tile_moe_tk_lin_silu_kernel(tc, xT, w8_words, w8_scales, w4_words, w4_scales
         add(low[1], part[1][0], part[1][1])
         pick(1, 3)
         add(three[1], low[1], part[1][2])
-        add(total[1], three[1], part[1][3])
-        store(1)
+        for t0 in (0, T // 2):
+            add(total[1], three[1], part[1][3], t0, t0 + T // 2)
+            store(1, t0, t0 + T // 2)

from contextlib import ExitStack

import concourse.mybir as mybir

K, T, E, C, N, TOP = 2560, 384, 12, 128, 256, 4
S = E * C
P = 128
PASSES, PASSES8 = 5, 2
PASSES4 = PASSES - PASSES8
HALVES = N // P
FLOPS = 2 * S * K * N
BYTES = 4 * K * T + E * N * (PASSES8 * (512 + 16) + PASSES4 * (256 + 16)) + 4 * N * E + 4 * TOP * T + 2 * P * (S + TOP * T) // 16 + 4 * N * T

F32 = mybir.dt.float32
BF16 = mybir.dt.bfloat16
I32 = mybir.dt.int32
U32 = mybir.dt.uint32
U16 = mybir.dt.uint16
U8 = mybir.dt.uint8
FP8X4 = mybir.dt.float8_e4m3fn_x4
FP4X4 = mybir.dt.float4_e2m1fn_x4
COPY = mybir.ActivationFunctionType.Copy
SILU = mybir.ActivationFunctionType.Silu
MULT = mybir.AluOpType.mult
ADD = mybir.AluOpType.add

WINDOW = 1024
PAD = WINDOW - T
PLANE_WINDOW = 1536
W8_ROW = 4
PLANE_ROW = (4, 12, 0, 8, 0)
PACK_OF = (0, 0, 0, 0, 1)
PACKS = 2
SHIFTED = 3
EARLY = 2
BATCHES = ((0, 4), (4, 8), (8, 12))


def tile_moe_tk_lin_silu_kernel(tc, xT, w8_words, w8_scales, w4_words, w4_scales, b, gate, offs, pos1, pos2, pos3, pos4, out):
    nc = tc.nc
    with ExitStack() as ctx:
        lists = ctx.enter_context(tc.tile_pool(name="lists", bufs=1))
        keep = ctx.enter_context(tc.tile_pool(name="keep", bufs=1))
        psum = ctx.enter_context(tc.psum_pool(name="psum", bufs=8))

        offs_sb = lists.tile([P, S // 16], U16, name="offs_sb")
        pos_sb = [lists.tile([P, T // 16], U16, name=f"pos_sb{r}") for r in range(TOP)]

        words = keep.tile([P, PASSES * T + PAD], I32, name="words", align_bytes=64)
        planes = keep.tile([P, (PACKS - 1) * T + PLANE_WINDOW], U8, name="planes", align_bytes=64)
        w8 = keep.tile([P, E * PASSES8, 4 * N], U8, name="w8", align_bytes=64)
        w4 = keep.tile([P, E * PASSES4, 2 * N], U8, name="w4", align_bytes=64)
        w8s = keep.tile([P, E * PASSES8, N], U8, name="w8s", align_bytes=64)
        w4s = keep.tile([P, E * PASSES4, N], U8, name="w4s", align_bytes=64)
        bias = keep.tile([P, HALVES, E], F32, name="bias")
        gates = keep.tile([P, TOP, T], F32, name="gates")
        raw = [keep.tile([P, 4, T], F32, name=f"raw{a}") for a in range(PASSES)]
        grouped = [keep.tile([P, T, 4], BF16, name=f"grouped{a}", align_bytes=64) for a in range(PASSES)]
        early_words = [keep.tile([P, S], U32, name=f"early_words{a}", align_bytes=64) for a in range(EARLY)]
        slot_planes = [keep.tile([P, S], U8, name=f"slot_planes{q}", align_bytes=64) for q in range(PACKS)]
        shifted = keep.tile([P, S], U8, name="shifted", align_bytes=64)
        y = [keep.tile([P, S], F32, name=f"y{h}") for h in range(HALVES)]
        dummy = keep.tile([P, 1], F32, name="dummy")

        x_rows = xT.rearrange("(a p j) t -> a p j t", p=P, j=4)
        nc.sync.dma_start(out=raw[0][:, :, 0:256], in_=x_rows[0][:, :, 0:256])
        nc.sync.dma_start(out=raw[0][:, :, 256:T], in_=x_rows[0][:, :, 256:T])
        nc.sync.dma_start(offs_sb[:], offs)

        nc.vector.memset(dummy[:], 0.0)
        nc.scalar.activation(dummy[:], dummy[:], SILU)
        nc.vector.memset(planes[:].bitcast(I32), 0)
        nc.vector.memset(words[:, PASSES * T :], 0)
        nc.vector.memset(w8s[:].rearrange("p e n -> p (e n)").bitcast(I32), 0)
        nc.vector.memset(w4s[:].rearrange("p e n -> p (e n)").bitcast(I32), 0)
        nc.vector.memset(shifted[:].bitcast(I32), 0)

        w8_rows = w8_words.rearrange("e a p n r -> p (e a) (n r)").bitcast(I32)
        w4_rows = w4_words.rearrange("e a p n -> p (e a) n").bitcast(I32)
        w8s_rows = w8_scales.rearrange("e a q n -> q (e a) n").bitcast(I32)
        w4s_rows = w4_scales.rearrange("e a q n -> q (e a) n").bitcast(I32)
        def load_w8(e0, e1):
            rows = slice(e0 * PASSES8, e1 * PASSES8)
            nc.sync.dma_start(out=w8[:, rows].bitcast(I32), in_=w8_rows[:, rows])

        def load_w4(e0, e1):
            rows = slice(e0 * PASSES4, e1 * PASSES4)
            nc.sync.dma_start(out=w4[:, rows].bitcast(I32), in_=w4_rows[:, rows])

        for r in range(4):
            nc.gpsimd.dma_start(out=w8s[W8_ROW + r : P : 32].bitcast(I32), in_=w8s_rows[r:16:4])
        for r in range(4):
            nc.gpsimd.dma_start(out=w4s[r:P:32].bitcast(I32), in_=w4s_rows[r:16:4])
        for a in range(1, PASSES):
            nc.sync.dma_start(out=raw[a][:], in_=x_rows[a])
        load_w8(0, 4)
        load_w4(0, 4)
        nc.sync.dma_start(out=bias[:], in_=b.rearrange("(h p) e -> p h e", p=P))
        load_w8(4, 8)
        load_w4(4, 8)
        for r, pos in enumerate((pos1, pos2, pos3, pos4)):
            nc.sync.dma_start(pos_sb[r][:], pos)
        load_w8(8, 12)
        load_w4(8, 12)
        for r in range(TOP):
            nc.sync.dma_start(out=gates[:, r, :], in_=gate[r, 0:P, :])

        def interleave_scalar(a, t0, t1):
            nc.scalar.activation(grouped[a][:, t0:t1, :], raw[a][:, :, t0:t1].rearrange("p j t -> p t j"), COPY)

        def interleave_vector(a, t0, t1):
            nc.vector.tensor_copy(out=grouped[a][:, t0:t1, :], in_=raw[a][:, :, t0:t1].rearrange("p j t -> p t j"))

        def word_column(a):
            return (PASSES - 1 - a) * T

        def plane_column(q):
            return (PACKS - 1 - q) * T

        def quantise(a):
            for t0, t1 in ((0, 256), (256, T)):
                w0, s0 = word_column(a), plane_column(PACK_OF[a])
                nc.vector.quantize_mx(
                    out=words[:, w0 + t0 : w0 + t1].bitcast(FP8X4),
                    scales=planes[PLANE_ROW[a] : P, s0 + t0 : s0 + t1],
                    in_=grouped[a][:, t0:t1, :].rearrange("p t j -> p (t j)"),
                )

        def gather_words(a, dst, j0, j1):
            w0 = word_column(a)
            nc.vector.tensor_copy(
                out=dst,
                in_=words[:, w0 : w0 + WINDOW].bitcast(U32).indirect(offs_sb[:, j0 // 16 : j1 // 16]),
            )

        def gather_planes(q, j0, j1):
            s0 = plane_column(q)
            nc.vector.tensor_copy(
                out=slot_planes[q][:, j0:j1],
                in_=planes[:, s0 : s0 + (WINDOW if j1 - j0 <= 512 else PLANE_WINDOW)].indirect(offs_sb[:, j0 // 16 : j1 // 16]),
            )

        def shift_planes(j0, j1):
            k = PLANE_ROW[SHIFTED]
            nc.gpsimd.dma_start(
                out=shifted[0:100, j0:j1].bitcast(I32),
                in_=slot_planes[PACK_OF[SHIFTED]][k : k + 100, j0:j1].bitcast(I32),
            )

        def multiply(acc, a, e, h, moving):
            cols = slice(e * C, (e + 1) * C)
            if a < PASSES8:
                i = e * PASSES8 + a
                lhsT = w8[:, i, 4 * P * h : 4 * P * (h + 1)].bitcast(FP8X4)
                lhsT_scale = w8s[W8_ROW:P, i, P * h : P * (h + 1)]
            else:
                i = e * PASSES4 + a - PASSES8
                lhsT = w4[:, i, 2 * P * h : 2 * P * (h + 1)].bitcast(FP4X4)
                lhsT_scale = w4s[:, i, P * h : P * (h + 1)]
            nc.tensor.matmul_mx(
                out=acc[:],
                lhsT=lhsT,
                lhsT_scale=lhsT_scale,
                rhs=moving.bitcast(FP8X4),
                rhs_scale=shifted[:, cols] if a == SHIFTED else slot_planes[PACK_OF[a]][PLANE_ROW[a] : P, cols],
                start=(a == 0),
                stop=(a == PASSES - 1),
            )

        interleave_scalar(0, 0, 128)
        interleave_vector(0, 128, 256)
        interleave_vector(0, 256, T)
        for a in range(1, PASSES):
            interleave_scalar(a, 0, T)
        quantise(0)
        for a in range(EARLY):
            for j in range(0, S, S // 2):
                gather_words(a, early_words[a][:, j : j + S // 2], j, j + S // 2)
            quantise(a + 1)
        quantise(3)

        for e0, e1 in BATCHES:
            j0, j1 = e0 * C, e1 * C
            if e0 == BATCHES[1][0]:
                gather_planes(0, j0, S)
                shift_planes(j0, S)
            if e0 > 0:
                gather_planes(1, j0, j1)
            batch_words = {a: early_words[a][:, j0:j1] for a in range(EARLY)}
            for a in range(EARLY, PASSES):
                tile = keep.tile([P, j1 - j0], U32, name=f"batch_words{a}", align_bytes=64)
                batch_words[a] = tile[:]
            gather_words(2, batch_words[2], j0, j1)
            if e0 == 0:
                gather_planes(0, j0, j1)
                shift_planes(j0, j1)
                quantise(4)
            gather_words(3, batch_words[3], j0, j1)
            if e0 == 0:
                gather_planes(1, j0, j1)
            accs = {}
            for e in range(e0, e1):
                for h in range(HALVES):
                    accs[e, h] = psum.tile([P, C], F32, name="acc")
            for a in range(PASSES - 1):
                for e in range(e0, e1):
                    for h in range(HALVES):
                        multiply(accs[e, h], a, e, h, batch_words[a][:, (e - e0) * C : (e - e0 + 1) * C])
            for f0, f1 in ((e0, e1),) if e1 < E else ((e0, e0 + 2), (e0 + 2, e0 + 3), (e0 + 3, e1)):
                gather_words(4, batch_words[4][:, (f0 - e0) * C : (f1 - e0) * C], f0 * C, f1 * C)
                for e in range(f0, f1):
                    for h in range(HALVES):
                        multiply(accs[e, h], 4, e, h, batch_words[4][:, (e - e0) * C : (e - e0 + 1) * C])
                        nc.scalar.activation(y[h][:, e * C : (e + 1) * C], accs[e, h][:], SILU, bias=bias[:, h, e : e + 1])

        part = [[keep.tile([P, T], F32, name=f"part{h}_{r}") for r in range(TOP)] for h in range(HALVES)]
        low = [keep.tile([P, T], F32, name=f"low{h}") for h in range(HALVES)]
        three = [keep.tile([P, T], F32, name=f"three{h}") for h in range(HALVES)]
        total = [keep.tile([P, T], F32, name=f"total{h}") for h in range(HALVES)]

        def pick(h, r):
            nc.vector.tensor_tensor(part[h][r][:], y[h][:].indirect(pos_sb[r][:]), gates[:, r, :], MULT)

        def add(dst, a, b, t0=0, t1=T):
            nc.vector.tensor_tensor(dst[:, t0:t1], a[:, t0:t1], b[:, t0:t1], ADD)

        def store(h, t0=0, t1=T):
            nc.sync.dma_start(out=out[h * P : (h + 1) * P, t0:t1], in_=total[h][:, t0:t1])

        pick(0, 0)
        pick(0, 1)
        pick(0, 2)
        add(low[0], part[0][0], part[0][1])
        pick(0, 3)
        add(three[0], low[0], part[0][2])
        pick(1, 0)
        add(total[0], three[0], part[0][3])
        store(0)
        pick(1, 1)
        pick(1, 2)
        add(low[1], part[1][0], part[1][1])
        pick(1, 3)
        add(three[1], low[1], part[1][2])
        for t0 in (0, T // 2):
            add(total[1], three[1], part[1][3], t0, t0 + T // 2)
            store(1, t0, t0 + T // 2)
